import numpy as np
import ml_dtypes


def mxq(x, axis, fmt="e4m3"):
    dtype, down = {"e4m3": (ml_dtypes.float8_e4m3fn, 7), "e5m2": (ml_dtypes.float8_e5m2, 14)}[fmt]
    v = np.moveaxis(np.asarray(x, np.float32).astype(ml_dtypes.bfloat16).astype(np.float64), axis, -1)
    blocks = v.reshape(v.shape[:-1] + (-1, 32))
    amax = np.abs(blocks).max(-1, keepdims=True)
    byte = np.maximum(np.where(amax > 0, np.frexp(amax)[1] - 1 + 127, 0) - down, 1)
    scale = np.exp2(byte - 127.0)
    codes = (blocks / scale).astype(np.float32).astype(dtype).astype(np.float64)
    return np.moveaxis((codes * scale).reshape(v.shape), -1, axis)


WIDE = False


def mx_kscale(k):
    if not WIDE:
        return np.ones(k)
    levels = np.array([10, -10, 5, -5, 0])
    if k % 512:
        return np.exp2(np.random.permutation(np.resize(levels, k // 32))).repeat(32)
    a = np.empty((k // 512, 16))
    for p in range(k // 512):
        a[p, :8] = np.random.permutation(np.resize(levels, 8))
        for g in range(8):
            far = levels[np.abs(levels - a[p, g]) >= 10]
            a[p, g + 8] = far[np.random.randint(len(far))]
    return np.exp2(a.ravel()).repeat(32)


def f64(x):
    return np.asarray(x).astype(np.float64)


def striped(idx):
    return np.tile(idx.reshape(-1, 16).T, (8, 1)).astype(np.uint16)


def unstriped(offs):
    return offs[:16].T.reshape(-1).astype(np.int64)


def pack_weight(w):
    k, n = w.shape
    w = f64(np.asarray(w, np.float32).astype(ml_dtypes.bfloat16)).reshape(k // 32, 32, n)
    amax = np.abs(w).max(1)
    byte = np.clip(np.where(amax > 0, np.frexp(amax)[1] - 1 + 127 - 7, 1), 1, 254)
    scaled = (w * np.exp2(127.0 - byte)[:, None, :]).reshape(k, n).astype(np.float32)
    words = np.ascontiguousarray(scaled.reshape(k // 512, 128, 4, n).transpose(0, 1, 3, 2)).astype(ml_dtypes.float8_e4m3fn).view(np.uint8)
    return words, np.ascontiguousarray(byte.astype(np.uint8).reshape(k // 512, 16, n))


def unpack_weight(words, scales):
    g, p, n, _ = words.shape
    vals = np.ascontiguousarray(words).view(ml_dtypes.float8_e4m3fn).astype(np.float64) * np.repeat(np.exp2(scales.astype(np.float64) - 127.0), 8, axis=1)[..., None]
    return vals.transpose(0, 1, 3, 2).reshape(g * 512, n)


K, T, E, C, N = 512, 2048, 16, 128, 512


def by_expert(wq, xq):
    return np.concatenate([wq[e].T @ xq[:, e * C:(e + 1) * C] for e in range(E)], axis=1)


def setup_inputs():
    n = np.random.standard_normal
    s = mx_kscale(K)[:, None]
    packed = [pack_weight(m) for m in n((E, K, N)) / np.sqrt(K) / s[None]]
    return {
        "xT": (n((K, T)) * s).astype(np.float32),
        "w_words": np.stack([m[0] for m in packed]),
        "w_scales": np.stack([m[1] for m in packed]),
        "gate": np.tile(np.random.uniform(0.2, 1.0, E * C), (N, 1)).astype(np.float32),
        "offs": striped(np.random.permutation(T)[:E * C]),
    }


def reference(xT, w_words, w_scales, gate, offs):
    idx = unstriped(offs)
    xq = mxq(f64(xT)[:, idx], 0, "e4m3")
    w = np.stack([unpack_weight(w_words[e], w_scales[e]) for e in range(E)])
    y = by_expert(w, xq)
    out = np.zeros((N, T))
    out[:, idx] = f64(gate) * y
    return out

@@ -1,0 +1,139 @@
+from contextlib import ExitStack
+
+import concourse.mybir as mybir
+
+K, T, E, C, N = 512, 2048, 16, 128, 512
+FLOPS = 2 * K * N * E * C
+BYTES = 4 * K * T + E * K * N + E * (K // 32) * N + 4 * E * C + 2 * 128 * (E * C // 16) + 4 * N * T
+
+F32 = mybir.dt.float32
+BF16 = mybir.dt.bfloat16
+U32 = mybir.dt.uint32
+I32 = mybir.dt.int32
+U16 = mybir.dt.uint16
+U8 = mybir.dt.uint8
+FP8X4 = mybir.dt.float8_e4m3fn_x4
+MULT = mybir.AluOpType.mult
+COPY = mybir.ActivationFunctionType.Copy
+
+P = 128
+GROUPS = 4
+EG = E // GROUPS
+SG = EG * C
+NB = N // P
+NCH = 4
+TC = T // NCH
+VECTOR_GROUPS = 2
+
+
+def tile_routed_moe_kernel(tc, xT, w_words, w_scales, gate, offs, out):
+    nc = tc.nc
+    with ExitStack() as ctx:
+        held = ctx.enter_context(tc.tile_pool(name="held", bufs=1))
+        psum = ctx.enter_context(tc.psum_pool(name="psum", bufs=8))
+
+        offs_t = held.tile([P, E * C // 16], U16, name="offs_t")
+        nc.sync.dma_start(offs_t[:], offs)
+
+        warm_in = held.tile([P, 1], F32, name="warm_in")
+        warm_out = held.tile([P, 1], F32, name="warm_out")
+        nc.vector.memset(warm_in[:], 0.0)
+        nc.scalar.copy(out=warm_out[:], in_=warm_in[:])
+
+        planes = held.tile([P, E * N], U8, name="planes", align_bytes=64)
+        nc.vector.memset(planes[:].bitcast(I32), 0)
+
+        x_view = xT.rearrange("(p t) n -> p t n", t=4)
+        raw = {}
+        for u in range(2):
+            for c in range(NCH):
+                r = held.tile([P, 2, TC], F32, name="raw%d_%d" % (u, c))
+                nc.sync.dma_start(r[:], x_view[:, 2 * u : 2 * u + 2, c * TC : (c + 1) * TC])
+                raw[(u, c)] = r
+
+        ws32 = w_scales.bitcast(I32)
+        for q in range(4):
+            nc.sync.dma_start(
+                planes[32 * q : 32 * q + 4, :].bitcast(I32).rearrange("r (e n) -> r e n", e=E),
+                ws32[:, 0, 4 * q : 4 * q + 4, :].rearrange("e r n -> r e n"),
+            )
+
+        ww32 = w_words.rearrange("e a p n r -> e a p (n r)").bitcast(I32)
+        wt = []
+        gt = []
+        for g in range(GROUPS):
+            w_g = held.tile([P, EG, N], U32, name="w%d" % g, align_bytes=64)
+            nc.sync.dma_start(w_g[:].bitcast(I32), ww32[g * EG : (g + 1) * EG, 0].rearrange("e p n -> p e n"))
+            wt.append(w_g)
+            g_g = held.tile([P, SG], F32, name="gate%d" % g)
+            nc.sync.dma_start(g_g[:], gate[0:P, g * SG : (g + 1) * SG])
+            gt.append(g_g)
+
+        win = [held.tile([P, 2 * T], BF16, name="win%d" % u) for u in range(2)]
+        planes23 = held.tile([P, 2, T], BF16, name="planes23")
+        for u in range(2):
+            for c in range(NCH):
+                dst = win[u][:, 2 * c * TC : 2 * (c + 1) * TC].rearrange("p (n e) -> p n e", e=2)
+                src = raw[(u, c)][:].rearrange("p e n -> p n e")
+                if u == 1:
+                    nc.gpsimd.tensor_copy(out=dst, in_=src)
+                    nc.scalar.copy(out=planes23[:, :, c * TC : (c + 1) * TC], in_=raw[(u, c)][:])
+                elif c % 2 == 1:
+                    nc.vector.tensor_copy(out=dst, in_=src)
+                else:
+                    nc.scalar.copy(out=dst, in_=src)
+
+        xi = [held.tile([P, 4 * SG], BF16, name="xi%d" % g, align_bytes=64) for g in range(GROUPS)]
+        codes = [held.tile([P, SG], U32, name="codes%d" % g, align_bytes=64) for g in range(GROUPS)]
+        xs = [held.tile([P, SG], U8, name="xs%d" % g, align_bytes=64) for g in range(GROUPS)]
+        wout = [held.tile([P, T], F32, name="wout%d" % b) for b in range(NB)]
+
+        def gather(u, g):
+            if u == 1 and g >= VECTOR_GROUPS:
+                for t in (2, 3):
+                    nc.scalar.activation(
+                        out=xi[g][:].rearrange("p (s t) -> p s t", t=4)[:, :, t],
+                        in_=planes23[:, t - 2, :].indirect(offs_t[:, g * (SG // 16) : (g + 1) * (SG // 16)]),
+                        func=COPY,
+                    )
+                return
+            nc.vector.tensor_copy(
+                out=xi[g][:].bitcast(U32).rearrange("p (s u) -> p s u", u=2)[:, :, u],
+                in_=win[u][:].bitcast(U32).indirect(offs_t[:, g * (SG // 16) : (g + 1) * (SG // 16)]),
+            )
+
+        def quantise(g):
+            nc.vector.quantize_mx(out=codes[g][:].bitcast(FP8X4), scales=xs[g][:], in_=xi[g][:])
+
+        for g in range(GROUPS):
+            gather(0, g)
+        gather(1, 0)
+        for g in range(GROUPS):
+            if g + 1 < GROUPS:
+                gather(1, g + 1)
+            quantise(g)
+
+        for g in range(GROUPS):
+            for b in range(NB):
+                acc = psum.tile([P, SG], F32, name="acc")
+                for j in range(EG):
+                    e = g * EG + j
+                    nc.tensor.matmul_mx(
+                        out=acc[:, j * C : (j + 1) * C],
+                        lhsT=wt[g][:, j, b * P : (b + 1) * P].bitcast(FP8X4),
+                        lhsT_scale=planes[:, e * N + b * P : e * N + (b + 1) * P],
+                        rhs=codes[g][:, j * C : (j + 1) * C].bitcast(FP8X4),
+                        rhs_scale=xs[g][:, j * C : (j + 1) * C],
+                        start=True,
+                        stop=True,
+                    )
+                y = held.tile([P, SG], F32, name="y%d_%d" % (g, b))
+                nc.scalar.copy(out=y[:], in_=acc[:])
+                nc.vector.tensor_tensor(
+                    out=wout[b][:].indirect(offs_t[:, g * (SG // 16) : (g + 1) * (SG // 16)]),
+                    in0=y[:],
+                    in1=gt[g][:],
+                    op=MULT,
+                )
+                if g == GROUPS - 1:
+                    nc.sync.dma_start(out[b * P : (b + 1) * P, :], wout[b][:])

@@ -17,13 +17,17 @@ MULT = mybir.AluOpType.mult
 COPY = mybir.ActivationFunctionType.Copy
 
 P = 128
-GROUPS = 4
-EG = E // GROUPS
-SG = EG * C
 NB = N // P
-NCH = 4
-TC = T // NCH
-VECTOR_GROUPS = 2
+SIZES = (512, 512, 512, 512)
+NG = len(SIZES)
+STARTS = [sum(SIZES[:g]) for g in range(NG)]
+PIECE = 512
+CASTS = (
+    (("v", 0, 1536), ("g", 1536, 2048)),
+    (("s", 0, 1152), ("g", 1152, 2048)),
+    (("v", 0, 1536), ("g", 1536, 2048)),
+    (("s", 0, 1152), ("g", 1152, 2048)),
+)
 
 
 def tile_routed_moe_kernel(tc, xT, w_words, w_scales, gate, offs, out):
@@ -40,100 +44,115 @@ def tile_routed_moe_kernel(tc, xT, w_words, w_scales, gate, offs, out):
         nc.vector.memset(warm_in[:], 0.0)
         nc.scalar.copy(out=warm_out[:], in_=warm_in[:])
 
-        planes = held.tile([P, E * N], U8, name="planes", align_bytes=64)
-        nc.vector.memset(planes[:].bitcast(I32), 0)
+        e_first = SIZES[0] // C
+        sc_a = held.tile([P, e_first * N], U8, name="sc_a", align_bytes=64)
+        sc_b = held.tile([P, (E - e_first) * N], U8, name="sc_b", align_bytes=64)
+        nc.vector.memset(sc_a[:].bitcast(I32), 0)
+        nc.vector.memset(sc_b[:].bitcast(I32), 0)
 
         x_view = xT.rearrange("(p t) n -> p t n", t=4)
-        raw = {}
-        for u in range(2):
-            for c in range(NCH):
-                r = held.tile([P, 2, TC], F32, name="raw%d_%d" % (u, c))
-                nc.sync.dma_start(r[:], x_view[:, 2 * u : 2 * u + 2, c * TC : (c + 1) * TC])
-                raw[(u, c)] = r
+        raw = held.tile([P, 4, T], F32, name="raw")
+        for t in range(4):
+            nc.sync.dma_start(raw[:, t, :], x_view[:, t, :])
 
         ws32 = w_scales.bitcast(I32)
-        for q in range(4):
-            nc.sync.dma_start(
-                planes[32 * q : 32 * q + 4, :].bitcast(I32).rearrange("r (e n) -> r e n", e=E),
-                ws32[:, 0, 4 * q : 4 * q + 4, :].rearrange("e r n -> r e n"),
-            )
-
         ww32 = w_words.rearrange("e a p n r -> e a p (n r)").bitcast(I32)
+
+        def load_scales(tile, e0, e1):
+            for q in range(4):
+                nc.sync.dma_start(
+                    tile[32 * q : 32 * q + 4, :].bitcast(I32).rearrange("r (e n) -> r e n", e=e1 - e0),
+                    ws32[e0:e1, 0, 4 * q : 4 * q + 4, :].rearrange("e r n -> r e n"),
+                )
+
         wt = []
         gt = []
-        for g in range(GROUPS):
-            w_g = held.tile([P, EG, N], U32, name="w%d" % g, align_bytes=64)
-            nc.sync.dma_start(w_g[:].bitcast(I32), ww32[g * EG : (g + 1) * EG, 0].rearrange("e p n -> p e n"))
+        for g in range(NG):
+            e0 = STARTS[g] // C
+            eg = SIZES[g] // C
+            if g == 0:
+                load_scales(sc_a, 0, e_first)
+            if g == 1:
+                load_scales(sc_b, e_first, E)
+            w_g = held.tile([P, eg, N], U32, name="w%d" % g, align_bytes=64)
+            nc.sync.dma_start(w_g[:].bitcast(I32), ww32[e0 : e0 + eg, 0].rearrange("e p n -> p e n"))
             wt.append(w_g)
-            g_g = held.tile([P, SG], F32, name="gate%d" % g)
-            nc.sync.dma_start(g_g[:], gate[0:P, g * SG : (g + 1) * SG])
+            g_g = held.tile([P, SIZES[g]], F32, name="gate%d" % g)
+            nc.sync.dma_start(g_g[:], gate[0:P, STARTS[g] : STARTS[g] + SIZES[g]])
             gt.append(g_g)
 
-        win = [held.tile([P, 2 * T], BF16, name="win%d" % u) for u in range(2)]
-        planes23 = held.tile([P, 2, T], BF16, name="planes23")
-        for u in range(2):
-            for c in range(NCH):
-                dst = win[u][:, 2 * c * TC : 2 * (c + 1) * TC].rearrange("p (n e) -> p n e", e=2)
-                src = raw[(u, c)][:].rearrange("p e n -> p n e")
-                if u == 1:
-                    nc.gpsimd.tensor_copy(out=dst, in_=src)
-                    nc.scalar.copy(out=planes23[:, :, c * TC : (c + 1) * TC], in_=raw[(u, c)][:])
-                elif c % 2 == 1:
-                    nc.vector.tensor_copy(out=dst, in_=src)
-                else:
-                    nc.scalar.copy(out=dst, in_=src)
-
-        xi = [held.tile([P, 4 * SG], BF16, name="xi%d" % g, align_bytes=64) for g in range(GROUPS)]
-        codes = [held.tile([P, SG], U32, name="codes%d" % g, align_bytes=64) for g in range(GROUPS)]
-        xs = [held.tile([P, SG], U8, name="xs%d" % g, align_bytes=64) for g in range(GROUPS)]
+        pl = held.tile([P, 4, T], BF16, name="pl")
+        xi = {g: held.tile([P, 4 * SIZES[g]], BF16, name="xi%d" % g, align_bytes=64) for g in range(2)}
+        codes = {}
+        xs = [held.tile([P, SIZES[g]], U8, name="xs%d" % g, align_bytes=64) for g in range(NG)]
         wout = [held.tile([P, T], F32, name="wout%d" % b) for b in range(NB)]
+        y = {}
 
-        def gather(u, g):
-            if u == 1 and g >= VECTOR_GROUPS:
-                for t in (2, 3):
-                    nc.scalar.activation(
-                        out=xi[g][:].rearrange("p (s t) -> p s t", t=4)[:, :, t],
-                        in_=planes23[:, t - 2, :].indirect(offs_t[:, g * (SG // 16) : (g + 1) * (SG // 16)]),
-                        func=COPY,
-                    )
-                return
+        def cols(s0, s1):
+            return offs_t[:, s0 // 16 : s1 // 16]
+
+        for t in range(4):
+            for eng, c0, c1 in CASTS[t]:
+                if eng == "v":
+                    nc.vector.tensor_copy(out=pl[:, t, c0:c1], in_=raw[:, t, c0:c1])
+                elif eng == "s":
+                    nc.scalar.copy(out=pl[:, t, c0:c1], in_=raw[:, t, c0:c1])
+                else:
+                    nc.gpsimd.tensor_copy(out=pl[:, t, c0:c1], in_=raw[:, t, c0:c1])
             nc.vector.tensor_copy(
-                out=xi[g][:].bitcast(U32).rearrange("p (s u) -> p s u", u=2)[:, :, u],
-                in_=win[u][:].bitcast(U32).indirect(offs_t[:, g * (SG // 16) : (g + 1) * (SG // 16)]),
+                out=xi[0][:].rearrange("p (s t) -> p s t", t=4)[:, :, t],
+                in_=raw[:, t, :].indirect(cols(0, SIZES[0])),
             )
 
-        def quantise(g):
+        def gathers(g):
+            if g >= 2:
+                xi[g] = held.tile([P, 4 * SIZES[g]], BF16, name="ring%d" % (g - 2), align_bytes=64)
+            for t in range(4):
+                for s in range(0, SIZES[g], PIECE):
+                    nc.scalar.activation(
+                        out=xi[g][:].rearrange("p (s t) -> p s t", t=4)[:, s : s + PIECE, t],
+                        in_=pl[:, t, :].indirect(cols(STARTS[g] + s, STARTS[g] + s + PIECE)),
+                        func=COPY,
+                    )
+
+        def products(g):
+            codes[g] = held.tile([P, SIZES[g]], U32, name="ring%d" % g, align_bytes=64)
             nc.vector.quantize_mx(out=codes[g][:].bitcast(FP8X4), scales=xs[g][:], in_=xi[g][:])
-
-        for g in range(GROUPS):
-            gather(0, g)
-        gather(1, 0)
-        for g in range(GROUPS):
-            if g + 1 < GROUPS:
-                gather(1, g + 1)
-            quantise(g)
-
-        for g in range(GROUPS):
             for b in range(NB):
-                acc = psum.tile([P, SG], F32, name="acc")
-                for j in range(EG):
-                    e = g * EG + j
+                acc = psum.tile([P, SIZES[g]], F32, name="acc")
+                for j in range(SIZES[g] // C):
+                    e = STARTS[g] // C + j
+                    if e < e_first:
+                        plane = sc_a[:, e * N + b * P : e * N + (b + 1) * P]
+                    else:
+                        plane = sc_b[:, (e - e_first) * N + b * P : (e - e_first) * N + (b + 1) * P]
                     nc.tensor.matmul_mx(
                         out=acc[:, j * C : (j + 1) * C],
                         lhsT=wt[g][:, j, b * P : (b + 1) * P].bitcast(FP8X4),
-                        lhsT_scale=planes[:, e * N + b * P : e * N + (b + 1) * P],
+                        lhsT_scale=plane,
                         rhs=codes[g][:, j * C : (j + 1) * C].bitcast(FP8X4),
                         rhs_scale=xs[g][:, j * C : (j + 1) * C],
                         start=True,
                         stop=True,
                     )
-                y = held.tile([P, SG], F32, name="y%d_%d" % (g, b))
-                nc.scalar.copy(out=y[:], in_=acc[:])
-                nc.vector.tensor_tensor(
-                    out=wout[b][:].indirect(offs_t[:, g * (SG // 16) : (g + 1) * (SG // 16)]),
-                    in0=y[:],
-                    in1=gt[g][:],
-                    op=MULT,
-                )
-                if g == GROUPS - 1:
-                    nc.sync.dma_start(out[b * P : (b + 1) * P, :], wout[b][:])
+                y_t = held.tile([P, SIZES[g]], F32, name="y%d_%d" % (g, b))
+                nc.scalar.copy(out=y_t[:], in_=acc[:])
+                y[(g, b)] = y_t
+
+        def scatter(g, b):
+            nc.vector.tensor_tensor(
+                out=wout[b][:].indirect(cols(STARTS[g], STARTS[g] + SIZES[g])),
+                in0=y[(g, b)][:],
+                in1=gt[g][:],
+                op=MULT,
+            )
+            if g == NG - 1:
+                nc.sync.dma_start(out[b * P : (b + 1) * P, :], wout[b][:])
+
+        products(0)
+        for g in range(NG):
+            if g + 1 < NG:
+                gathers(g + 1)
+                products(g + 1)
+            for b in range(NB):
+                scatter(g, b)

@@ -65,18 +65,23 @@ def tile_routed_moe_kernel(tc, xT, w_words, w_scales, gate, offs, out):
                     ws32[e0:e1, 0, 4 * q : 4 * q + 4, :].rearrange("e r n -> r e n"),
                 )
 
-        wt = []
+        wt = {}
         gt = []
-        for g in range(NG):
+
+        def load_weights(g):
             e0 = STARTS[g] // C
             eg = SIZES[g] // C
+            w_g = held.tile([P, eg, N], U32, name="w_first" if g == 0 else "w_next", align_bytes=64)
+            nc.sync.dma_start(w_g[:].bitcast(I32), ww32[e0 : e0 + eg, 0].rearrange("e p n -> p e n"))
+            wt[g] = w_g
+
+        for g in range(NG):
             if g == 0:
                 load_scales(sc_a, 0, e_first)
             if g == 1:
                 load_scales(sc_b, e_first, E)
-            w_g = held.tile([P, eg, N], U32, name="w%d" % g, align_bytes=64)
-            nc.sync.dma_start(w_g[:].bitcast(I32), ww32[e0 : e0 + eg, 0].rearrange("e p n -> p e n"))
-            wt.append(w_g)
+            if g < 2:
+                load_weights(g)
             g_g = held.tile([P, SIZES[g]], F32, name="gate%d" % g)
             nc.sync.dma_start(g_g[:], gate[0:P, STARTS[g] : STARTS[g] + SIZES[g]])
             gt.append(g_g)
@@ -116,6 +121,8 @@ def tile_routed_moe_kernel(tc, xT, w_words, w_scales, gate, offs, out):
                     )
 
         def products(g):
+            if g >= 2:
+                load_weights(g)
             codes[g] = held.tile([P, SIZES[g]], U32, name="ring%d" % g, align_bytes=64)
             nc.vector.quantize_mx(out=codes[g][:].bitcast(FP8X4), scales=xs[g][:], in_=xi[g][:])
             for b in range(NB):

@@ -71,20 +71,30 @@ def tile_routed_moe_kernel(tc, xT, w_words, w_scales, gate, offs, out):
         def load_weights(g):
             e0 = STARTS[g] // C
             eg = SIZES[g] // C
-            w_g = held.tile([P, eg, N], U32, name="w_first" if g == 0 else "w_next", align_bytes=64)
+            w_g = held.tile([P, eg, N], U32, name="w_next", align_bytes=64)
             nc.sync.dma_start(w_g[:].bitcast(I32), ww32[e0 : e0 + eg, 0].rearrange("e p n -> p e n"))
             wt[g] = w_g
 
-        for g in range(NG):
-            if g == 0:
-                load_scales(sc_a, 0, e_first)
-            if g == 1:
-                load_scales(sc_b, e_first, E)
-            if g < 2:
-                load_weights(g)
+        def load_first_weights(b):
+            w_b = held.tile([P, e_first, P], U32, name="w_first%d" % b, align_bytes=64)
+            nc.sync.dma_start(w_b[:].bitcast(I32), ww32[0:e_first, 0, :, b * P : (b + 1) * P].rearrange("e p n -> p e n"))
+            w_first.append(w_b)
+
+        def load_gate(g):
             g_g = held.tile([P, SIZES[g]], F32, name="gate%d" % g)
             nc.sync.dma_start(g_g[:], gate[0:P, STARTS[g] : STARTS[g] + SIZES[g]])
             gt.append(g_g)
+
+        w_first = []
+        load_scales(sc_a, 0, e_first)
+        load_first_weights(0)
+        load_gate(0)
+        for b in range(1, NB):
+            load_first_weights(b)
+        load_scales(sc_b, e_first, E)
+        load_weights(1)
+        for g in range(1, NG):
+            load_gate(g)
 
         pl = held.tile([P, 4, T], BF16, name="pl")
         xi = {g: held.tile([P, 4 * SIZES[g]], BF16, name="xi%d" % g, align_bytes=64) for g in range(2)}
@@ -135,7 +145,7 @@ def tile_routed_moe_kernel(tc, xT, w_words, w_scales, gate, offs, out):
                         plane = sc_b[:, (e - e_first) * N + b * P : (e - e_first) * N + (b + 1) * P]
                     nc.tensor.matmul_mx(
                         out=acc[:, j * C : (j + 1) * C],
-                        lhsT=wt[g][:, j, b * P : (b + 1) * P].bitcast(FP8X4),
+                        lhsT=(w_first[b][:, j, :] if g == 0 else wt[g][:, j, b * P : (b + 1) * P]).bitcast(FP8X4),
                         lhsT_scale=plane,
                         rhs=codes[g][:, j * C : (j + 1) * C].bitcast(FP8X4),
                         rhs_scale=xs[g][:, j * C : (j + 1) * C],

@@ -23,10 +23,10 @@ NG = len(SIZES)
 STARTS = [sum(SIZES[:g]) for g in range(NG)]
 PIECE = 512
 CASTS = (
-    (("v", 0, 1536), ("g", 1536, 2048)),
-    (("s", 0, 1152), ("g", 1152, 2048)),
-    (("v", 0, 1536), ("g", 1536, 2048)),
-    (("s", 0, 1152), ("g", 1152, 2048)),
+    (("v", 0, 1024), ("v", 1024, 2048)),
+    (("g", 0, 1024), ("s", 1024, 2048)),
+    (("g", 0, 1024), ("v", 1024, 2048)),
+    (("g", 0, 1024), ("s", 1024, 2048)),
 )
 
 
@@ -53,7 +53,8 @@ def tile_routed_moe_kernel(tc, xT, w_words, w_scales, gate, offs, out):
         x_view = xT.rearrange("(p t) n -> p t n", t=4)
         raw = held.tile([P, 4, T], F32, name="raw")
         for t in range(4):
-            nc.sync.dma_start(raw[:, t, :], x_view[:, t, :])
+            for h in range(2):
+                nc.sync.dma_start(raw[:, t, h * (T // 2) : (h + 1) * (T // 2)], x_view[:, t, h * (T // 2) : (h + 1) * (T // 2)])
 
         ws32 = w_scales.bitcast(I32)
         ww32 = w_words.rearrange("e a p n r -> e a p (n r)").bitcast(I32)

@@ -23,10 +23,10 @@ NG = len(SIZES)
 STARTS = [sum(SIZES[:g]) for g in range(NG)]
 PIECE = 512
 CASTS = (
-    (("v", 0, 1024), ("v", 1024, 2048)),
-    (("g", 0, 1024), ("s", 1024, 2048)),
+    (("v", 0, 512), ("g", 512, 1024), ("v", 1024, 1536), ("s", 1536, 2048)),
+    (("g", 0, 1024), ("v", 1024, 1536), ("s", 1536, 2048)),
     (("g", 0, 1024), ("v", 1024, 2048)),
-    (("g", 0, 1024), ("s", 1024, 2048)),
+    (("g", 0, 512), ("v", 512, 1024), ("s", 1024, 1536), ("g", 1536, 2048)),
 )
 
 

from contextlib import ExitStack

import concourse.mybir as mybir

K, T, E, C, N = 512, 2048, 16, 128, 512
FLOPS = 2 * K * N * E * C
BYTES = 4 * K * T + E * K * N + E * (K // 32) * N + 4 * E * C + 2 * 128 * (E * C // 16) + 4 * N * T

F32 = mybir.dt.float32
BF16 = mybir.dt.bfloat16
U32 = mybir.dt.uint32
I32 = mybir.dt.int32
U16 = mybir.dt.uint16
U8 = mybir.dt.uint8
FP8X4 = mybir.dt.float8_e4m3fn_x4
MULT = mybir.AluOpType.mult
COPY = mybir.ActivationFunctionType.Copy

P = 128
NB = N // P
SIZES = (512, 512, 512, 512)
NG = len(SIZES)
STARTS = [sum(SIZES[:g]) for g in range(NG)]
PIECE = 512
CASTS = (
    (("v", 0, 512), ("g", 512, 1024), ("v", 1024, 1536), ("s", 1536, 2048)),
    (("g", 0, 1024), ("v", 1024, 1536), ("s", 1536, 2048)),
    (("g", 0, 1024), ("v", 1024, 2048)),
    (("g", 0, 512), ("v", 512, 1024), ("s", 1024, 1536), ("g", 1536, 2048)),
)


def tile_routed_moe_kernel(tc, xT, w_words, w_scales, gate, offs, out):
    nc = tc.nc
    with ExitStack() as ctx:
        held = ctx.enter_context(tc.tile_pool(name="held", bufs=1))
        psum = ctx.enter_context(tc.psum_pool(name="psum", bufs=8))

        offs_t = held.tile([P, E * C // 16], U16, name="offs_t")
        nc.sync.dma_start(offs_t[:], offs)

        warm_in = held.tile([P, 1], F32, name="warm_in")
        warm_out = held.tile([P, 1], F32, name="warm_out")
        nc.vector.memset(warm_in[:], 0.0)
        nc.scalar.copy(out=warm_out[:], in_=warm_in[:])

        e_first = SIZES[0] // C
        sc_a = held.tile([P, e_first * N], U8, name="sc_a", align_bytes=64)
        sc_b = held.tile([P, (E - e_first) * N], U8, name="sc_b", align_bytes=64)
        nc.vector.memset(sc_a[:].bitcast(I32), 0)
        nc.vector.memset(sc_b[:].bitcast(I32), 0)

        x_view = xT.rearrange("(p t) n -> p t n", t=4)
        raw = held.tile([P, 4, T], F32, name="raw")
        for t in range(4):
            for h in range(2):
                nc.sync.dma_start(raw[:, t, h * (T // 2) : (h + 1) * (T // 2)], x_view[:, t, h * (T // 2) : (h + 1) * (T // 2)])

        ws32 = w_scales.bitcast(I32)
        ww32 = w_words.rearrange("e a p n r -> e a p (n r)").bitcast(I32)

        def load_scales(tile, e0, e1):
            for q in range(4):
                nc.sync.dma_start(
                    tile[32 * q : 32 * q + 4, :].bitcast(I32).rearrange("r (e n) -> r e n", e=e1 - e0),
                    ws32[e0:e1, 0, 4 * q : 4 * q + 4, :].rearrange("e r n -> r e n"),
                )

        wt = {}
        gt = []

        def load_weights(g):
            e0 = STARTS[g] // C
            eg = SIZES[g] // C
            w_g = held.tile([P, eg, N], U32, name="w_next", align_bytes=64)
            nc.sync.dma_start(w_g[:].bitcast(I32), ww32[e0 : e0 + eg, 0].rearrange("e p n -> p e n"))
            wt[g] = w_g

        def load_first_weights(b):
            w_b = held.tile([P, e_first, P], U32, name="w_first%d" % b, align_bytes=64)
            nc.sync.dma_start(w_b[:].bitcast(I32), ww32[0:e_first, 0, :, b * P : (b + 1) * P].rearrange("e p n -> p e n"))
            w_first.append(w_b)

        def load_gate(g):
            g_g = held.tile([P, SIZES[g]], F32, name="gate%d" % g)
            nc.sync.dma_start(g_g[:], gate[0:P, STARTS[g] : STARTS[g] + SIZES[g]])
            gt.append(g_g)

        w_first = []
        load_scales(sc_a, 0, e_first)
        load_first_weights(0)
        load_gate(0)
        for b in range(1, NB):
            load_first_weights(b)
        load_scales(sc_b, e_first, E)
        load_weights(1)
        for g in range(1, NG):
            load_gate(g)

        pl = held.tile([P, 4, T], BF16, name="pl")
        xi = {g: held.tile([P, 4 * SIZES[g]], BF16, name="xi%d" % g, align_bytes=64) for g in range(2)}
        codes = {}
        xs = [held.tile([P, SIZES[g]], U8, name="xs%d" % g, align_bytes=64) for g in range(NG)]
        wout = [held.tile([P, T], F32, name="wout%d" % b) for b in range(NB)]
        y = {}

        def cols(s0, s1):
            return offs_t[:, s0 // 16 : s1 // 16]

        for t in range(4):
            for eng, c0, c1 in CASTS[t]:
                if eng == "v":
                    nc.vector.tensor_copy(out=pl[:, t, c0:c1], in_=raw[:, t, c0:c1])
                elif eng == "s":
                    nc.scalar.copy(out=pl[:, t, c0:c1], in_=raw[:, t, c0:c1])
                else:
                    nc.gpsimd.tensor_copy(out=pl[:, t, c0:c1], in_=raw[:, t, c0:c1])
            nc.vector.tensor_copy(
                out=xi[0][:].rearrange("p (s t) -> p s t", t=4)[:, :, t],
                in_=raw[:, t, :].indirect(cols(0, SIZES[0])),
            )

        def gathers(g):
            if g >= 2:
                xi[g] = held.tile([P, 4 * SIZES[g]], BF16, name="ring%d" % (g - 2), align_bytes=64)
            for t in range(4):
                for s in range(0, SIZES[g], PIECE):
                    nc.scalar.activation(
                        out=xi[g][:].rearrange("p (s t) -> p s t", t=4)[:, s : s + PIECE, t],
                        in_=pl[:, t, :].indirect(cols(STARTS[g] + s, STARTS[g] + s + PIECE)),
                        func=COPY,
                    )

        def products(g):
            if g >= 2:
                load_weights(g)
            codes[g] = held.tile([P, SIZES[g]], U32, name="ring%d" % g, align_bytes=64)
            nc.vector.quantize_mx(out=codes[g][:].bitcast(FP8X4), scales=xs[g][:], in_=xi[g][:])
            for b in range(NB):
                acc = psum.tile([P, SIZES[g]], F32, name="acc")
                for j in range(SIZES[g] // C):
                    e = STARTS[g] // C + j
                    if e < e_first:
                        plane = sc_a[:, e * N + b * P : e * N + (b + 1) * P]
                    else:
                        plane = sc_b[:, (e - e_first) * N + b * P : (e - e_first) * N + (b + 1) * P]
                    nc.tensor.matmul_mx(
                        out=acc[:, j * C : (j + 1) * C],
                        lhsT=(w_first[b][:, j, :] if g == 0 else wt[g][:, j, b * P : (b + 1) * P]).bitcast(FP8X4),
                        lhsT_scale=plane,
                        rhs=codes[g][:, j * C : (j + 1) * C].bitcast(FP8X4),
                        rhs_scale=xs[g][:, j * C : (j + 1) * C],
                        start=True,
                        stop=True,
                    )
                y_t = held.tile([P, SIZES[g]], F32, name="y%d_%d" % (g, b))
                nc.scalar.copy(out=y_t[:], in_=acc[:])
                y[(g, b)] = y_t

        def scatter(g, b):
            nc.vector.tensor_tensor(
                out=wout[b][:].indirect(cols(STARTS[g], STARTS[g] + SIZES[g])),
                in0=y[(g, b)][:],
                in1=gt[g][:],
                op=MULT,
            )
            if g == NG - 1:
                nc.sync.dma_start(out[b * P : (b + 1) * P, :], wout[b][:])

        products(0)
        for g in range(NG):
            if g + 1 < NG:
                gathers(g + 1)
                products(g + 1)
            for b in range(NB):
                scatter(g, b)
